import numpy as np, ml_dtypes
CORES = [78,86,94,102,110,118]
N = 6
import mx_ref
NC, G = 128, 2
C = np.float32(0.023)
BF = ml_dtypes.bfloat16
def cut(t, i, w=512):
    return t[:, w * i:w * i + w]
def tile(rs):
    return np.stack(rs, axis=2).reshape(128, -1).astype(BF)
def layer(w, X):
    out = []
    for i in range(G):
        for t in range(len(X)):
            p = mx_ref.matmul(mx_ref.quantize(cut(w, len(X) * i + t)), X[t])
            z = p if t == 0 else z + p
        out.append(z)
    return out
def act(Z):
    return [np.maximum(s * z, 0) * C for z in Z for s in (1, -1)]
def setup_inputs(rng):
    def f(*shape):
        return mx_ref.flush((rng.standard_normal(shape, dtype=np.float32) * np.exp2(rng.integers(-2, 3, shape[:-1] + (1,)))).astype(BF))
    return {"x": f(N, 128, 4 * NC), "w1": f(N, 128, G * 512), "w2": f(N, 128, 512)}
def setup_inputs_blocks(rng):
    d = setup_inputs(rng)
    for k in ("x", "w1", "w2"): d[k] = mx_ref.spread(d[k], rng, 2)
    return d
def setup_inputs_wide(rng):
    d = setup_inputs(rng)
    for k in ("x", "w1", "w2"): d[k] = mx_ref.flush((d[k].astype(np.float32) * np.exp2(rng.integers(-6, 7, (N, 1, 1))).astype(np.float32)).astype(BF))
    return d
def reference(x, w1, w2):
    X = [mx_ref.quantize(x[j]) for j in range(N)]
    y = np.zeros((N, 128, NC), np.float32)
    for c in range(N):
        for r in range(N):
            p = mx_ref.matmul(mx_ref.quantize(w2[r]), mx_ref.quantize(tile(act(layer(w1[r], [X[c]])))))
            y[c] = p if r == 0 else y[c] + p
    return {"y": y}

@@ -1,0 +1,187 @@
+from concourse.bass import DstId, RemoteDMATransfer
+from concourse.mybir import dt, AluOpType, ActivationFunctionType
+
+F8 = "float8_e4m3fn_x4"
+C = 0.023
+COLS = (128, 256, 256, 128)
+
+SCRATCH = {
+    "xb": ("sbuf", [128, 512], "bfloat16"),
+    "w1b": ("sbuf", [128, 1024], "bfloat16"),
+    "w2b": ("sbuf", [128, 512], "bfloat16"),
+    "xq": ("sbuf", [128, 128], F8), "xs": ("sbuf", [128, 128], "uint8"),
+    "fq": ("sbuf", [128, 256], F8), "fs": ("sbuf", [128, 256], "uint8"),
+    "wq": ("sbuf", [128, 384], F8), "ws": ("sbuf", [128, 384], "uint8"),
+    "mq": ("sbuf", [128, 384], F8), "ms": ("sbuf", [128, 384], "uint8"),
+    "part0": ("sbuf", [128, 128], "float32"), "part1": ("sbuf", [128, 128], "float32"),
+    "land0": ("sbuf", [128, 128], "float32"), "land1": ("sbuf", [128, 128], "float32"),
+    "acc": ("sbuf", [128, 128], "float32"), "yv": ("sbuf", [128, 128], "float32"),
+}
+for _k, _n in enumerate(COLS):
+    SCRATCH["h%d" % _k] = ("sbuf", [128, 4 * _n], "bfloat16")
+    SCRATCH["hq%d" % _k] = ("sbuf", [128, _n], F8)
+    SCRATCH["hs%d" % _k] = ("sbuf", [128, _n], "uint8")
+for _k in range(8):
+    SCRATCH["b%d" % _k] = ("psum", [128, 512], "float32")
+
+SEMAPHORES = ["lx", "lw1", "lw2", "qx", "qw1", "qw2", "ax", "aw1", "aw2", "ay0", "ay1", "sent",
+              "p0", "p1", "pown", "c0", "c1", "added", "yd", "st"]
+for _k in range(4):
+    SEMAPHORES += ["z0_%d" % _k, "z1_%d" % _k, "rv%d" % _k, "rs%d" % _k, "qh%d" % _k]
+
+
+def plan(T, topo):
+    chips = [topo.chip(c) for c in T.cores]
+    n = len(chips)
+    group = [[j for j in range(n) if j == i or topo.same_plane(chips[i], chips[j])] for i in range(n)]
+    partner = {}
+    for i in range(n):
+        for j in range(n):
+            if topo.mates(chips[i], chips[j]):
+                partner[i] = j
+    for i in range(n):
+        if i not in partner:
+            j = [k for k in range(n) if k not in partner and k not in group[i]][0]
+            partner[i], partner[j] = j, i
+    return group, partner
+
+
+def rank_program(g, core, T, topo):
+    rank = T.rank_of(core)
+    if rank is None:
+        return
+    s = T.sem
+    group, partner = plan(T, topo)
+
+    def others(i):
+        return [j for j in group[i] if j != i]
+
+    def dst_id(j):
+        a = topo.addr(T.cores[j])
+        return DstId(rid=a[0], pnc=a[1])
+
+    def engines(dsts):
+        m = topo.mask(core, T.cores[dsts[0]])
+        for j in dsts:
+            m &= topo.mask(core, T.cores[j])
+        return m
+
+    mine = others(rank)
+    mate = partner[rank]
+    slot = [others(j).index(rank) for j in mine]
+
+    g.sync.dma_start(T.xb[:], T.x[:]).then_inc(s.lx, 16)
+    g.scalar.dma_start(T.w1b[:], T.w1[:]).then_inc(s.lw1, 16)
+    g.sync.dma_start(T.w2b[:], T.w2[:]).then_inc(s.lw2, 16)
+
+    v = g.vector
+    v.wait_ge(s.lx, 16)
+    v.quantize_mx(T.xq[:], T.xs[:], T.xb[:]).then_inc(s.qx, 1)
+    v.wait_ge(s.lw1, 16)
+    v.quantize_mx(T.wq[:, 0:256], T.ws[:, 0:256], T.w1b[:]).then_inc(s.qw1, 1)
+    v.wait_ge(s.lw2, 16)
+    v.quantize_mx(T.wq[:, 256:384], T.ws[:, 256:384], T.w2b[:]).then_inc(s.qw2, 1)
+
+    def cast(src, dsts, ids, sem):
+        m = engines(ids)
+        g.remote_dma_fused([RemoteDMATransfer(srcs=[src], dsts=dsts, dst_ids=[dst_id(j) for j in ids],
+                                              dma_engine_mask=m, remote_sem=sem, alu_op=0)], local_sem=s.sent)
+        return bin(m).count("1")
+
+    n_sent, n_x, n_w1 = 0, 0, 0
+    g.wait_ge(s.qx, 1)
+    k = cast(T.xq[:].bitcast(dt.uint8), [T.fq[:, 128 * a:128 * a + 128].bitcast(dt.uint8) for a in slot], mine, s.ax)
+    n_sent, n_x = n_sent + k, n_x + k
+    k = cast(T.xs[:], [T.fs[:, 128 * a:128 * a + 128] for a in slot], mine, s.ax)
+    n_sent, n_x = n_sent + k, n_x + k
+    g.wait_ge(s.qw1, 1)
+    k = cast(T.wq[:, 0:256].bitcast(dt.uint8), [T.mq[:, 0:256].bitcast(dt.uint8)], [mate], s.aw1)
+    n_sent, n_w1 = n_sent + k, n_w1 + k
+    g.wait_ge(s.qw2, 1)
+    k = cast(T.ws[:], [T.ms[:]], [mate], s.aw1)
+    n_sent, n_w1 = n_sent + k, n_w1 + k
+    n_w2 = cast(T.wq[:, 256:384].bitcast(dt.uint8), [T.mq[:, 256:384].bitcast(dt.uint8)], [mate], s.aw2)
+    n_sent += n_w2
+
+    g.wait_ge(s.c0, 1)
+    g.wait_ge(s.c1, 1)
+    both = engines(mine)
+    bits = [1 << e for e in range(both.bit_length()) if both >> e & 1]
+    half = len(bits) // 2
+    g.remote_dma_fused([RemoteDMATransfer(srcs=[T["part%d" % a][:]], dsts=[T["land%d" % slot[a]][:]],
+                                          dst_ids=[dst_id(mine[a])], dma_engine_mask=sum(bits[a::2]),
+                                          remote_sem=s["ay%d" % slot[a]], alu_op=0)
+                        for a in range(2)], local_sem=s.sent)
+    n_sent += 2 * half
+    g.wait_ge(s.sent, n_sent)
+
+    t = g.tensor
+    zbank = ((T.b0, T.b1), (T.b2, T.b3), (T.b4, T.b5), (T.b1, T.b2))
+    pown, pf = T.b6, (T.b7, T.b0)
+    own, far = (T.wq, T.ws), (T.mq, T.ms)
+
+    def first(k, w, x):
+        n = COLS[k]
+        for i in range(2):
+            t.matmul_mx(zbank[k][i][:, 0:n], w[0][:, 128 * i:128 * i + 128], w[1][:, 128 * i:128 * i + 128],
+                        x[0][:], x[1][:], True, True).then_inc(s["z%d_%d" % (i, k)], 1)
+
+    def second(out, k, a, w, start):
+        hq, hs = T["hq%d" % k], T["hs%d" % k]
+        return t.matmul_mx(out[:, 0:128], w[0][:, 256:384], w[1][:, 256:384],
+                           hq[:, 128 * a:128 * a + 128], hs[:, 128 * a:128 * a + 128], start, not start)
+
+    t.wait_ge(s.qx, 1)
+    t.wait_ge(s.qw1, 1)
+    first(0, own, (T.xq, T.xs))
+    t.wait_ge(s.ax, 2 * n_x)
+    first(1, own, (T.fq, T.fs))
+    t.wait_ge(s.qw2, 1)
+    t.wait_ge(s.qh0, 1)
+    second(pown, 0, 0, own, True)
+    t.wait_ge(s.aw1, n_w1)
+    first(2, far, (T.fq, T.fs))
+    t.wait_ge(s.qh1, 1)
+    for a in range(2):
+        second(pf[a], 1, a, own, True)
+    first(3, far, (T.xq, T.xs))
+    t.wait_ge(s.qh2, 1)
+    t.wait_ge(s.aw2, n_w2)
+    for a in range(2):
+        second(pf[a], 2, a, far, False).then_inc(s["p%d" % a], 1)
+    t.wait_ge(s.qh3, 1)
+    second(pown, 3, 0, far, False).then_inc(s.pown, 1)
+
+    sc = g.scalar
+    RELU, COPY = ActivationFunctionType.Relu, ActivationFunctionType.Copy
+
+    def tile(k):
+        n, h = COLS[k], T["h%d" % k]
+        v.wait_ge(s["z0_%d" % k], 1)
+        for b, c in ((0, C), (1, -C)):
+            v.tensor_scalar(h[:, b:4 * n:4], zbank[k][0][:, 0:n], c, 0.0, AluOpType.mult, AluOpType.max).then_inc(s["rv%d" % k], 1)
+        sc.wait_ge(s["z1_%d" % k], 1)
+        for b, c in ((2, C), (3, -C)):
+            sc.activation(h[:, b:4 * n:4], zbank[k][1][:, 0:n], RELU, scale=c).then_inc(s["rs%d" % k], 1)
+        v.wait_ge(s["rv%d" % k], 2)
+        v.wait_ge(s["rs%d" % k], 2)
+        v.quantize_mx(T["hq%d" % k][:], T["hs%d" % k][:], h[:]).then_inc(s["qh%d" % k], 1)
+
+    tile(0)
+    tile(1)
+    tile(2)
+    sc.wait_ge(s.p0, 1)
+    sc.activation(T.part0[:], pf[0][:, 0:128], COPY).then_inc(s.c0, 1)
+    v.wait_ge(s.p1, 1)
+    v.tensor_copy(T.part1[:], pf[1][:, 0:128]).then_inc(s.c1, 1)
+    tile(3)
+
+    v.wait_ge(s.pown, 1)
+    v.wait_ge(s.ay0, half)
+    v.tensor_tensor(T.acc[:], pown[:, 0:128], T.land0[:], AluOpType.add).then_inc(s.added, 1)
+    v.wait_ge(s.added, 1)
+    v.wait_ge(s.ay1, half)
+    v.tensor_tensor(T.yv[:], T.acc[:], T.land1[:], AluOpType.add).then_inc(s.yd, 1)
+    g.sync.wait_ge(s.yd, 1)
+    g.sync.dma_start(T.y[:], T.yv[:]).then_inc(s.st, 16)
+    g.sync.wait_ge(s.st, 16)

@@ -3,7 +3,7 @@ from concourse.mybir import dt, AluOpType, ActivationFunctionType
 
 F8 = "float8_e4m3fn_x4"
 C = 0.023
-COLS = (128, 256, 256, 128)
+BLOCKS = 6
 
 SCRATCH = {
     "xb": ("sbuf", [128, 512], "bfloat16"),
@@ -17,16 +17,16 @@ SCRATCH = {
     "land0": ("sbuf", [128, 128], "float32"), "land1": ("sbuf", [128, 128], "float32"),
     "acc": ("sbuf", [128, 128], "float32"), "yv": ("sbuf", [128, 128], "float32"),
 }
-for _k, _n in enumerate(COLS):
-    SCRATCH["h%d" % _k] = ("sbuf", [128, 4 * _n], "bfloat16")
-    SCRATCH["hq%d" % _k] = ("sbuf", [128, _n], F8)
-    SCRATCH["hs%d" % _k] = ("sbuf", [128, _n], "uint8")
+for _k in range(BLOCKS):
+    SCRATCH["h%d" % _k] = ("sbuf", [128, 512], "bfloat16")
+    SCRATCH["hq%d" % _k] = ("sbuf", [128, 128], F8)
+    SCRATCH["hs%d" % _k] = ("sbuf", [128, 128], "uint8")
 for _k in range(8):
     SCRATCH["b%d" % _k] = ("psum", [128, 512], "float32")
 
-SEMAPHORES = ["lx", "lw1", "lw2", "qx", "qw1", "qw2", "ax", "aw1", "aw2", "ay0", "ay1", "sent",
-              "p0", "p1", "pown", "c0", "c1", "added", "yd", "st"]
-for _k in range(4):
+SEMAPHORES = ["lx", "lw1", "lw2", "qx", "qw1", "qw2", "ax0", "ax1", "ax2", "aw1", "aw2", "ay0", "ay1", "sent",
+              "hop0", "hop1", "p0", "p1", "pown", "c0", "c1", "added", "yd", "st"]
+for _k in range(BLOCKS):
     SEMAPHORES += ["z0_%d" % _k, "z1_%d" % _k, "rv%d" % _k, "rs%d" % _k, "qh%d" % _k]
 
 
@@ -34,7 +34,7 @@ def plan(T, topo):
     chips = [topo.chip(c) for c in T.cores]
     n = len(chips)
     group = [[j for j in range(n) if j == i or topo.same_plane(chips[i], chips[j])] for i in range(n)]
-    partner = {}
+    partner, helper = {}, {}
     for i in range(n):
         for j in range(n):
             if topo.mates(chips[i], chips[j]):
@@ -43,145 +43,204 @@ def plan(T, topo):
         if i not in partner:
             j = [k for k in range(n) if k not in partner and k not in group[i]][0]
             partner[i], partner[j] = j, i
-    return group, partner
+    for i in range(n):
+        if not topo.mates(chips[i], chips[partner[i]]):
+            c = T.cores[i]
+            helper[i] = [k for k in range(128) if topo.chip(k) == chips[i] and topo.die(k) != topo.die(c)
+                         and topo.may_write(k, T.cores[partner[i]])][0]
+    return group, partner, helper
+
+
+def count(mask):
+    return bin(mask).count("1")
+
+
+def send(g, topo, src, dsts, cores, mask, sem, sent):
+    ids = []
+    for c in cores:
+        a = topo.addr(c)
+        ids.append(DstId(rid=a[0], pnc=a[1]))
+    g.remote_dma_fused([RemoteDMATransfer(srcs=[src], dsts=dsts, dst_ids=ids, dma_engine_mask=mask, remote_sem=sem,
+                                          alu_op=0)], local_sem=sent)
+    return count(mask)
+
+
+def codes(buf, a, b):
+    return buf[:, a:b].bitcast(dt.uint8)
+
+
+def relay_pieces(q, sc):
+    return [codes(q, 256, 384), sc[:, 256:384]]
+
+
+def helper_program(g, core, T, topo, src, dst):
+    s = T.sem
+    k = count(topo.mask(src, core) & ~topo.mask(src, dst))
+    n = 0
+    for i, piece in enumerate(relay_pieces(T.mq, T.ms)):
+        g.wait_ge(s["hop%d" % i], k)
+        n += send(g, topo, piece, [piece], [dst], topo.mask(core, dst), s.aw2, s.sent)
+    g.wait_ge(s.sent, n)
 
 
 def rank_program(g, core, T, topo):
     rank = T.rank_of(core)
-    if rank is None:
-        return
     s = T.sem
-    group, partner = plan(T, topo)
+    group, partner, helper = plan(T, topo)
+    if rank is None:
+        for i in helper:
+            if helper[i] == core:
+                helper_program(g, core, T, topo, T.cores[i], T.cores[partner[i]])
+        return
 
     def others(i):
-        return [j for j in group[i] if j != i]
+        a = group[i].index(i)
+        return group[i][a + 1:] + group[i][:a]
 
-    def dst_id(j):
-        a = topo.addr(T.cores[j])
-        return DstId(rid=a[0], pnc=a[1])
-
-    def engines(dsts):
-        m = topo.mask(core, T.cores[dsts[0]])
-        for j in dsts:
-            m &= topo.mask(core, T.cores[j])
-        return m
+    def ax(i):
+        return s["ax%d" % group[i].index(i)]
 
     mine = others(rank)
-    mate = partner[rank]
+    peers = [T.cores[j] for j in mine]
+    far_core = T.cores[partner[rank]]
     slot = [others(j).index(rank) for j in mine]
+    early, late = (1, 0) if mine[0] in helper else (0, 1)
+    relayed = rank in helper
 
     g.sync.dma_start(T.xb[:], T.x[:]).then_inc(s.lx, 16)
-    g.scalar.dma_start(T.w1b[:], T.w1[:]).then_inc(s.lw1, 16)
-    g.sync.dma_start(T.w2b[:], T.w2[:]).then_inc(s.lw2, 16)
+    if relayed:
+        g.scalar.dma_start(T.w2b[:], T.w2[:]).then_inc(s.lw2, 16)
+        g.sync.dma_start(T.w1b[:], T.w1[:]).then_inc(s.lw1, 16)
+    else:
+        g.scalar.dma_start(T.w1b[:], T.w1[:]).then_inc(s.lw1, 16)
+        g.sync.dma_start(T.w2b[:], T.w2[:]).then_inc(s.lw2, 16)
 
     v = g.vector
     v.wait_ge(s.lx, 16)
     v.quantize_mx(T.xq[:], T.xs[:], T.xb[:]).then_inc(s.qx, 1)
-    v.wait_ge(s.lw1, 16)
-    v.quantize_mx(T.wq[:, 0:256], T.ws[:, 0:256], T.w1b[:]).then_inc(s.qw1, 1)
-    v.wait_ge(s.lw2, 16)
-    v.quantize_mx(T.wq[:, 256:384], T.ws[:, 256:384], T.w2b[:]).then_inc(s.qw2, 1)
 
-    def cast(src, dsts, ids, sem):
-        m = engines(ids)
-        g.remote_dma_fused([RemoteDMATransfer(srcs=[src], dsts=dsts, dst_ids=[dst_id(j) for j in ids],
-                                              dma_engine_mask=m, remote_sem=sem, alu_op=0)], local_sem=s.sent)
-        return bin(m).count("1")
+    def pack_w1():
+        v.wait_ge(s.lw1, 16)
+        v.quantize_mx(T.wq[:, 0:256], T.ws[:, 0:256], T.w1b[:]).then_inc(s.qw1, 1)
 
-    n_sent, n_x, n_w1 = 0, 0, 0
+    def pack_w2():
+        v.wait_ge(s.lw2, 16)
+        v.quantize_mx(T.wq[:, 256:384], T.ws[:, 256:384], T.w2b[:]).then_inc(s.qw2, 1)
+
+    if relayed:
+        pack_w2()
+        pack_w1()
+    else:
+        pack_w1()
+        pack_w2()
+
+    mp = topo.mask(core, peers[0]) & topo.mask(core, peers[1])
+    mf = topo.mask(core, far_core)
+    n_x, n_w = count(mp), count(mf)
+    sent = []
+
+    def to_peers(src, dsts):
+        sent.append(send(g, topo, src, dsts, peers, mp, ax(rank), s.sent))
+
+    def to_partner(src, dst, sem):
+        sent.append(send(g, topo, src, [dst], [far_core], mf, sem, s.sent))
+
+    def hop(i):
+        h = helper[rank]
+        sent.append(send(g, topo, relay_pieces(T.wq, T.ws)[i], [relay_pieces(T.mq, T.ms)[i]], [h],
+                         topo.mask(core, h) & ~mf, s["hop%d" % i], s.sent))
+
     g.wait_ge(s.qx, 1)
-    k = cast(T.xq[:].bitcast(dt.uint8), [T.fq[:, 128 * a:128 * a + 128].bitcast(dt.uint8) for a in slot], mine, s.ax)
-    n_sent, n_x = n_sent + k, n_x + k
-    k = cast(T.xs[:], [T.fs[:, 128 * a:128 * a + 128] for a in slot], mine, s.ax)
-    n_sent, n_x = n_sent + k, n_x + k
-    g.wait_ge(s.qw1, 1)
-    k = cast(T.wq[:, 0:256].bitcast(dt.uint8), [T.mq[:, 0:256].bitcast(dt.uint8)], [mate], s.aw1)
-    n_sent, n_w1 = n_sent + k, n_w1 + k
-    g.wait_ge(s.qw2, 1)
-    k = cast(T.ws[:], [T.ms[:]], [mate], s.aw1)
-    n_sent, n_w1 = n_sent + k, n_w1 + k
-    n_w2 = cast(T.wq[:, 256:384].bitcast(dt.uint8), [T.mq[:, 256:384].bitcast(dt.uint8)], [mate], s.aw2)
-    n_sent += n_w2
+    to_peers(codes(T.xq, 0, 128), [codes(T.fq, 128 * a, 128 * a + 128) for a in slot])
+    to_peers(T.xs[:], [T.fs[:, 128 * a:128 * a + 128] for a in slot])
+    if relayed:
+        g.wait_ge(s.qw2, 1)
+        hop(0)
+        g.wait_ge(s.qw1, 1)
+        to_partner(codes(T.wq, 0, 256), codes(T.mq, 0, 256), s.aw1)
+        to_partner(T.ws[:, 0:256], T.ms[:, 0:256], s.aw1)
+        hop(1)
+        n_w2 = 2 * count(topo.mask(helper[partner[rank]], core))
+    else:
+        g.wait_ge(s.qw1, 1)
+        to_partner(codes(T.wq, 0, 256), codes(T.mq, 0, 256), s.aw1)
+        g.wait_ge(s.qw2, 1)
+        to_partner(T.ws[:], T.ms[:], s.aw1)
+        to_partner(codes(T.wq, 256, 384), codes(T.mq, 256, 384), s.aw2)
+        n_w2 = n_w
 
-    g.wait_ge(s.c0, 1)
-    g.wait_ge(s.c1, 1)
-    both = engines(mine)
-    bits = [1 << e for e in range(both.bit_length()) if both >> e & 1]
-    half = len(bits) // 2
-    g.remote_dma_fused([RemoteDMATransfer(srcs=[T["part%d" % a][:]], dsts=[T["land%d" % slot[a]][:]],
-                                          dst_ids=[dst_id(mine[a])], dma_engine_mask=sum(bits[a::2]),
-                                          remote_sem=s["ay%d" % slot[a]], alu_op=0)
-                        for a in range(2)], local_sem=s.sent)
-    n_sent += 2 * half
-    g.wait_ge(s.sent, n_sent)
+    for a in range(2):
+        g.wait_ge(s["c%d" % a], 1)
+        sent.append(send(g, topo, T["part%d" % a][:], [T["land%d" % slot[a]][:]], [peers[a]], mp, s["ay%d" % slot[a]], s.sent))
+    g.wait_ge(s.sent, sum(sent))
 
     t = g.tensor
-    zbank = ((T.b0, T.b1), (T.b2, T.b3), (T.b4, T.b5), (T.b1, T.b2))
-    pown, pf = T.b6, (T.b7, T.b0)
+    zbank = {0: (T.b0, T.b1), 1 + early: (T.b2, T.b3), 1 + late: (T.b4, T.b5), 3: (T.b6, T.b7), 4: (T.b2, T.b3), 5: (T.b5, T.b6)}
+    pown, pf = T.b0, (T.b1, T.b4)
     own, far = (T.wq, T.ws), (T.mq, T.ms)
 
-    def first(k, w, x):
-        n = COLS[k]
+    def first(k, w, x, a=0):
         for i in range(2):
-            t.matmul_mx(zbank[k][i][:, 0:n], w[0][:, 128 * i:128 * i + 128], w[1][:, 128 * i:128 * i + 128],
-                        x[0][:], x[1][:], True, True).then_inc(s["z%d_%d" % (i, k)], 1)
+            t.matmul_mx(zbank[k][i][:, 0:128], w[0][:, 128 * i:128 * i + 128], w[1][:, 128 * i:128 * i + 128],
+                        x[0][:, 128 * a:128 * a + 128], x[1][:, 128 * a:128 * a + 128], True, True).then_inc(s["z%d_%d" % (i, k)], 1)
 
-    def second(out, k, a, w, start):
-        hq, hs = T["hq%d" % k], T["hs%d" % k]
+    def second(out, k, w, start):
         return t.matmul_mx(out[:, 0:128], w[0][:, 256:384], w[1][:, 256:384],
-                           hq[:, 128 * a:128 * a + 128], hs[:, 128 * a:128 * a + 128], start, not start)
+                           T["hq%d" % k][:], T["hs%d" % k][:], start, not start)
 
     t.wait_ge(s.qx, 1)
     t.wait_ge(s.qw1, 1)
     first(0, own, (T.xq, T.xs))
-    t.wait_ge(s.ax, 2 * n_x)
-    first(1, own, (T.fq, T.fs))
+    for a in (early, late):
+        t.wait_ge(ax(mine[a]), 2 * n_x)
+        first(1 + a, own, (T.fq, T.fs), a)
     t.wait_ge(s.qw2, 1)
     t.wait_ge(s.qh0, 1)
-    second(pown, 0, 0, own, True)
-    t.wait_ge(s.aw1, n_w1)
-    first(2, far, (T.fq, T.fs))
-    t.wait_ge(s.qh1, 1)
+    second(pown, 0, own, True)
+    t.wait_ge(s.aw1, 2 * n_w)
+    first(3, far, (T.fq, T.fs), 0)
+    t.wait_ge(s["qh%d" % (1 + early)], 1)
+    first(4, far, (T.fq, T.fs), 1)
+    t.wait_ge(s["qh%d" % (1 + late)], 1)
     for a in range(2):
-        second(pf[a], 1, a, own, True)
-    first(3, far, (T.xq, T.xs))
-    t.wait_ge(s.qh2, 1)
+        second(pf[a], 1 + a, own, True)
     t.wait_ge(s.aw2, n_w2)
     for a in range(2):
-        second(pf[a], 2, a, far, False).then_inc(s["p%d" % a], 1)
-    t.wait_ge(s.qh3, 1)
-    second(pown, 3, 0, far, False).then_inc(s.pown, 1)
+        t.wait_ge(s["qh%d" % (3 + a)], 1)
+        second(pf[a], 3 + a, far, False).then_inc(s["p%d" % a], 1)
+    first(5, far, (T.xq, T.xs))
+    t.wait_ge(s.qh5, 1)
+    second(pown, 5, far, False).then_inc(s.pown, 1)
 
     sc = g.scalar
     RELU, COPY = ActivationFunctionType.Relu, ActivationFunctionType.Copy
 
     def tile(k):
-        n, h = COLS[k], T["h%d" % k]
+        h = T["h%d" % k]
         v.wait_ge(s["z0_%d" % k], 1)
         for b, c in ((0, C), (1, -C)):
-            v.tensor_scalar(h[:, b:4 * n:4], zbank[k][0][:, 0:n], c, 0.0, AluOpType.mult, AluOpType.max).then_inc(s["rv%d" % k], 1)
+            v.tensor_scalar(h[:, b:512:4], zbank[k][0][:, 0:128], c, 0.0, AluOpType.mult, AluOpType.max).then_inc(s["rv%d" % k], 1)
         sc.wait_ge(s["z1_%d" % k], 1)
         for b, c in ((2, C), (3, -C)):
-            sc.activation(h[:, b:4 * n:4], zbank[k][1][:, 0:n], RELU, scale=c).then_inc(s["rs%d" % k], 1)
+            sc.activation(h[:, b:512:4], zbank[k][1][:, 0:128], RELU, scale=c).then_inc(s["rs%d" % k], 1)
         v.wait_ge(s["rv%d" % k], 2)
         v.wait_ge(s["rs%d" % k], 2)
         v.quantize_mx(T["hq%d" % k][:], T["hs%d" % k][:], h[:]).then_inc(s["qh%d" % k], 1)
 
-    tile(0)
-    tile(1)
-    tile(2)
+    for k in (0, 1 + early, 1 + late, 3, 4):
+        tile(k)
     sc.wait_ge(s.p0, 1)
     sc.activation(T.part0[:], pf[0][:, 0:128], COPY).then_inc(s.c0, 1)
     v.wait_ge(s.p1, 1)
     v.tensor_copy(T.part1[:], pf[1][:, 0:128]).then_inc(s.c1, 1)
-    tile(3)
+    tile(5)
 
     v.wait_ge(s.pown, 1)
-    v.wait_ge(s.ay0, half)
-    v.tensor_tensor(T.acc[:], pown[:, 0:128], T.land0[:], AluOpType.add).then_inc(s.added, 1)
+    v.wait_ge(s["ay%d" % early], n_x)
+    v.tensor_tensor(T.acc[:], pown[:, 0:128], T["land%d" % early][:], AluOpType.add).then_inc(s.added, 1)
     v.wait_ge(s.added, 1)
-    v.wait_ge(s.ay1, half)
-    v.tensor_tensor(T.yv[:], T.acc[:], T.land1[:], AluOpType.add).then_inc(s.yd, 1)
+    v.wait_ge(s["ay%d" % late], n_x)
+    v.tensor_tensor(T.yv[:], T.acc[:], T["land%d" % late][:], AluOpType.add).then_inc(s.yd, 1)
     g.sync.wait_ge(s.yd, 1)
     g.sync.dma_start(T.y[:], T.yv[:]).then_inc(s.st, 16)
     g.sync.wait_ge(s.st, 16)

@@ -3,7 +3,8 @@ from concourse.mybir import dt, AluOpType, ActivationFunctionType
 
 F8 = "float8_e4m3fn_x4"
 C = 0.023
-BLOCKS = 6
+BLOCKS = ["oo", "oa", "ob", "pa", "pb", "po"]
+PIECES = ["xac", "xas", "xbc", "xbs", "w1c0", "w1c1", "w2c", "w1s", "w2s"]
 
 SCRATCH = {
     "xb": ("sbuf", [128, 512], "bfloat16"),
@@ -17,230 +18,210 @@ SCRATCH = {
     "land0": ("sbuf", [128, 128], "float32"), "land1": ("sbuf", [128, 128], "float32"),
     "acc": ("sbuf", [128, 128], "float32"), "yv": ("sbuf", [128, 128], "float32"),
 }
-for _k in range(BLOCKS):
-    SCRATCH["h%d" % _k] = ("sbuf", [128, 512], "bfloat16")
-    SCRATCH["hq%d" % _k] = ("sbuf", [128, 128], F8)
-    SCRATCH["hs%d" % _k] = ("sbuf", [128, 128], "uint8")
+SEMAPHORES = ["lx", "lw1", "lw2", "qx", "qw1", "qw2", "ay0", "ay1", "sent", "hop_xbs", "hop_xbc", "p0", "p1",
+              "pown", "c0", "c1", "added", "yd", "st"]
+SEMAPHORES += ["in_" + _p for _p in PIECES]
+for _k in BLOCKS:
+    SCRATCH["h" + _k] = ("sbuf", [128, 512], "bfloat16")
+    SCRATCH["hq" + _k] = ("sbuf", [128, 128], F8)
+    SCRATCH["hs" + _k] = ("sbuf", [128, 128], "uint8")
+    SEMAPHORES += [_n + _k for _n in ("z0", "z1", "r0", "r1", "qh")]
 for _k in range(8):
     SCRATCH["b%d" % _k] = ("psum", [128, 512], "float32")
-
-SEMAPHORES = ["lx", "lw1", "lw2", "qx", "qw1", "qw2", "ax0", "ax1", "ax2", "aw1", "aw2", "ay0", "ay1", "sent",
-              "hop0", "hop1", "p0", "p1", "pown", "c0", "c1", "added", "yd", "st"]
-for _k in range(BLOCKS):
-    SEMAPHORES += ["z0_%d" % _k, "z1_%d" % _k, "rv%d" % _k, "rs%d" % _k, "qh%d" % _k]
 
 
 def plan(T, topo):
     chips = [topo.chip(c) for c in T.cores]
     n = len(chips)
     group = [[j for j in range(n) if j == i or topo.same_plane(chips[i], chips[j])] for i in range(n)]
+    nxt = [group[i][(group[i].index(i) + 1) % len(group[i])] for i in range(n)]
+    prv = [group[i][group[i].index(i) - 1] for i in range(n)]
     partner, helper = {}, {}
     for i in range(n):
         for j in range(n):
             if topo.mates(chips[i], chips[j]):
                 partner[i] = j
+    left = [i for i in range(n) if i not in partner]
+    for i in left:
+        partner[i] = [j for j in left if j not in group[i]][0]
     for i in range(n):
-        if i not in partner:
-            j = [k for k in range(n) if k not in partner and k not in group[i]][0]
-            partner[i], partner[j] = j, i
-    for i in range(n):
-        if not topo.mates(chips[i], chips[partner[i]]):
-            c = T.cores[i]
-            helper[i] = [k for k in range(128) if topo.chip(k) == chips[i] and topo.die(k) != topo.die(c)
-                         and topo.may_write(k, T.cores[partner[i]])][0]
-    return group, partner, helper
+        c = T.cores[i]
+        helper[i] = [k for k in range(128) if topo.chip(k) == chips[i] and topo.die(k) != topo.die(c)
+                     and topo.may_write(k, T.cores[prv[i]])][0]
+    return nxt, prv, partner, helper
 
 
 def count(mask):
     return bin(mask).count("1")
 
 
-def send(g, topo, src, dsts, cores, mask, sem, sent):
-    ids = []
-    for c in cores:
-        a = topo.addr(c)
-        ids.append(DstId(rid=a[0], pnc=a[1]))
-    g.remote_dma_fused([RemoteDMATransfer(srcs=[src], dsts=dsts, dst_ids=ids, dma_engine_mask=mask, remote_sem=sem,
-                                          alu_op=0)], local_sem=sent)
-    return count(mask)
-
-
 def codes(buf, a, b):
     return buf[:, a:b].bitcast(dt.uint8)
 
 
-def relay_pieces(q, sc):
-    return [codes(q, 256, 384), sc[:, 256:384]]
-
-
-def helper_program(g, core, T, topo, src, dst):
-    s = T.sem
-    k = count(topo.mask(src, core) & ~topo.mask(src, dst))
-    n = 0
-    for i, piece in enumerate(relay_pieces(T.mq, T.ms)):
-        g.wait_ge(s["hop%d" % i], k)
-        n += send(g, topo, piece, [piece], [dst], topo.mask(core, dst), s.aw2, s.sent)
-    g.wait_ge(s.sent, n)
+def piece(T, p):
+    return {"xac": (codes(T.xq, 0, 128), codes(T.fq, 0, 128)), "xas": (T.xs[:], T.fs[:, 0:128]),
+            "xbc": (codes(T.xq, 0, 128), codes(T.fq, 128, 256)), "xbs": (T.xs[:], T.fs[:, 128:256]),
+            "w1c0": (codes(T.wq, 0, 128), codes(T.mq, 0, 128)), "w1c1": (codes(T.wq, 128, 256), codes(T.mq, 128, 256)),
+            "w2c": (codes(T.wq, 256, 384), codes(T.mq, 256, 384)),
+            "w1s": (T.ws[:, 0:256], T.ms[:, 0:256]), "w2s": (T.ws[:, 256:384], T.ms[:, 256:384])}[p]
 
 
 def rank_program(g, core, T, topo):
     rank = T.rank_of(core)
     s = T.sem
-    group, partner, helper = plan(T, topo)
+    nxt, prv, partner, helper = plan(T, topo)
+    sent = []
+
+    def send(*writes):
+        transfers = []
+        for src, dst, dest, mask, sem in writes:
+            a = topo.addr(dest)
+            transfers.append(RemoteDMATransfer(srcs=[src], dsts=[dst], dst_ids=[DstId(rid=a[0], pnc=a[1])],
+                                               dma_engine_mask=mask, remote_sem=sem, alu_op=0))
+            sent.append(count(mask))
+        g.remote_dma_fused(transfers, local_sem=s.sent)
+
+    def hop_mask(i):
+        free = topo.mask(T.cores[i], helper[i]) & ~topo.mask(T.cores[i], T.cores[partner[i]])
+        return sum([1 << e for e in range(free.bit_length()) if free >> e & 1][::2])
+
     if rank is None:
         for i in helper:
             if helper[i] == core:
-                helper_program(g, core, T, topo, T.cores[i], T.cores[partner[i]])
+                dest = T.cores[prv[i]]
+                for p in ("xbs", "xbc"):
+                    place = piece(T, p)[1]
+                    g.wait_ge(s["hop_" + p], count(hop_mask(i)))
+                    send((place, place, dest, topo.mask(core, dest), s["in_" + p]))
+                g.wait_ge(s.sent, sum(sent))
         return
 
-    def others(i):
-        a = group[i].index(i)
-        return group[i][a + 1:] + group[i][:a]
-
-    def ax(i):
-        return s["ax%d" % group[i].index(i)]
-
-    mine = others(rank)
-    peers = [T.cores[j] for j in mine]
-    far_core = T.cores[partner[rank]]
-    slot = [others(j).index(rank) for j in mine]
-    early, late = (1, 0) if mine[0] in helper else (0, 1)
-    relayed = rank in helper
+    next_core, prev_core, far_core = T.cores[nxt[rank]], T.cores[prv[rank]], T.cores[partner[rank]]
 
     g.sync.dma_start(T.xb[:], T.x[:]).then_inc(s.lx, 16)
-    if relayed:
-        g.scalar.dma_start(T.w2b[:], T.w2[:]).then_inc(s.lw2, 16)
-        g.sync.dma_start(T.w1b[:], T.w1[:]).then_inc(s.lw1, 16)
-    else:
-        g.scalar.dma_start(T.w1b[:], T.w1[:]).then_inc(s.lw1, 16)
-        g.sync.dma_start(T.w2b[:], T.w2[:]).then_inc(s.lw2, 16)
+    g.scalar.dma_start(T.w1b[:], T.w1[:]).then_inc(s.lw1, 16)
+    g.sync.dma_start(T.w2b[:], T.w2[:]).then_inc(s.lw2, 16)
 
-    v = g.vector
-    v.wait_ge(s.lx, 16)
-    v.quantize_mx(T.xq[:], T.xs[:], T.xb[:]).then_inc(s.qx, 1)
+    def give(p, dest):
+        src, dst = piece(T, p)
+        return src, dst, dest, topo.mask(core, dest), s["in_" + p]
 
-    def pack_w1():
-        v.wait_ge(s.lw1, 16)
-        v.quantize_mx(T.wq[:, 0:256], T.ws[:, 0:256], T.w1b[:]).then_inc(s.qw1, 1)
-
-    def pack_w2():
-        v.wait_ge(s.lw2, 16)
-        v.quantize_mx(T.wq[:, 256:384], T.ws[:, 256:384], T.w2b[:]).then_inc(s.qw2, 1)
-
-    if relayed:
-        pack_w2()
-        pack_w1()
-    else:
-        pack_w1()
-        pack_w2()
-
-    mp = topo.mask(core, peers[0]) & topo.mask(core, peers[1])
-    mf = topo.mask(core, far_core)
-    n_x, n_w = count(mp), count(mf)
-    sent = []
-
-    def to_peers(src, dsts):
-        sent.append(send(g, topo, src, dsts, peers, mp, ax(rank), s.sent))
-
-    def to_partner(src, dst, sem):
-        sent.append(send(g, topo, src, [dst], [far_core], mf, sem, s.sent))
-
-    def hop(i):
-        h = helper[rank]
-        sent.append(send(g, topo, relay_pieces(T.wq, T.ws)[i], [relay_pieces(T.mq, T.ms)[i]], [h],
-                         topo.mask(core, h) & ~mf, s["hop%d" % i], s.sent))
+    def hop(p):
+        src, dst = piece(T, p)
+        return src, dst, helper[rank], hop_mask(rank), s["hop_" + p]
 
     g.wait_ge(s.qx, 1)
-    to_peers(codes(T.xq, 0, 128), [codes(T.fq, 128 * a, 128 * a + 128) for a in slot])
-    to_peers(T.xs[:], [T.fs[:, 128 * a:128 * a + 128] for a in slot])
-    if relayed:
-        g.wait_ge(s.qw2, 1)
-        hop(0)
-        g.wait_ge(s.qw1, 1)
-        to_partner(codes(T.wq, 0, 256), codes(T.mq, 0, 256), s.aw1)
-        to_partner(T.ws[:, 0:256], T.ms[:, 0:256], s.aw1)
-        hop(1)
-        n_w2 = 2 * count(topo.mask(helper[partner[rank]], core))
-    else:
-        g.wait_ge(s.qw1, 1)
-        to_partner(codes(T.wq, 0, 256), codes(T.mq, 0, 256), s.aw1)
-        g.wait_ge(s.qw2, 1)
-        to_partner(T.ws[:], T.ms[:], s.aw1)
-        to_partner(codes(T.wq, 256, 384), codes(T.mq, 256, 384), s.aw2)
-        n_w2 = n_w
-
-    for a in range(2):
+    send(hop("xbs"))
+    send(give("xac", next_core), hop("xbc"))
+    send(give("xas", next_core))
+    g.wait_ge(s.qw1, 1)
+    for p in ("w1c0", "w1s", "w1c1"):
+        send(give(p, far_core))
+    g.wait_ge(s.qw2, 1)
+    for p in ("w2c", "w2s"):
+        send(give(p, far_core))
+    for a, dest in ((0, prev_core), (1, next_core)):
         g.wait_ge(s["c%d" % a], 1)
-        sent.append(send(g, topo, T["part%d" % a][:], [T["land%d" % slot[a]][:]], [peers[a]], mp, s["ay%d" % slot[a]], s.sent))
+        send((T["part%d" % a][:], T["land%d" % a][:], dest, topo.mask(core, dest), s["ay%d" % a]))
     g.wait_ge(s.sent, sum(sent))
 
     t = g.tensor
-    zbank = {0: (T.b0, T.b1), 1 + early: (T.b2, T.b3), 1 + late: (T.b4, T.b5), 3: (T.b6, T.b7), 4: (T.b2, T.b3), 5: (T.b5, T.b6)}
-    pown, pf = T.b0, (T.b1, T.b4)
     own, far = (T.wq, T.ws), (T.mq, T.ms)
+    zbank = {"oo": (T.b0, T.b1), "oa": (T.b2, T.b3), "pa": (T.b4, T.b5), "ob": (T.b6, T.b7), "pb": (T.b1, T.b2),
+             "po": (T.b6, T.b7)}
+    pown, pf = T.b0, (T.b3, T.b4)
 
-    def first(k, w, x, a=0):
-        for i in range(2):
+    def landed(*names):
+        for p in names:
+            sender = {"xa": prev_core, "xb": helper[nxt[rank]]}.get(p[:2], far_core)
+            t.wait_ge(s["in_" + p], count(topo.mask(sender, core)))
+
+    def rows_read(i, k):
+        t.wait_ge(s["r%d%s" % (i, k)], 2)
+
+    def first(k, tiles=(0, 1)):
+        w = own if k[0] == "o" else far
+        x = {"o": (T.xq[:], T.xs[:]), "a": (T.fq[:, 0:128], T.fs[:, 0:128]), "b": (T.fq[:, 128:256], T.fs[:, 128:256])}[k[1]]
+        for i in tiles:
             t.matmul_mx(zbank[k][i][:, 0:128], w[0][:, 128 * i:128 * i + 128], w[1][:, 128 * i:128 * i + 128],
-                        x[0][:, 128 * a:128 * a + 128], x[1][:, 128 * a:128 * a + 128], True, True).then_inc(s["z%d_%d" % (i, k)], 1)
+                        x[0], x[1], True, True).then_inc(s["z%d%s" % (i, k)], 1)
 
-    def second(out, k, w, start):
-        return t.matmul_mx(out[:, 0:128], w[0][:, 256:384], w[1][:, 256:384],
-                           T["hq%d" % k][:], T["hs%d" % k][:], start, not start)
+    def second(out, k, start):
+        w = own if k[0] == "o" else far
+        t.wait_ge(s["qh" + k], 1)
+        return t.matmul_mx(out[:, 0:128], w[0][:, 256:384], w[1][:, 256:384], T["hq" + k][:], T["hs" + k][:], start, not start)
 
     t.wait_ge(s.qx, 1)
     t.wait_ge(s.qw1, 1)
-    first(0, own, (T.xq, T.xs))
-    for a in (early, late):
-        t.wait_ge(ax(mine[a]), 2 * n_x)
-        first(1 + a, own, (T.fq, T.fs), a)
+    first("oo")
+    landed("xac", "xas")
+    first("oa")
+    landed("w1c0", "w1s")
+    first("pa", (0,))
+    landed("w1c1")
+    first("pa", (1,))
     t.wait_ge(s.qw2, 1)
-    t.wait_ge(s.qh0, 1)
-    second(pown, 0, own, True)
-    t.wait_ge(s.aw1, 2 * n_w)
-    first(3, far, (T.fq, T.fs), 0)
-    t.wait_ge(s["qh%d" % (1 + early)], 1)
-    first(4, far, (T.fq, T.fs), 1)
-    t.wait_ge(s["qh%d" % (1 + late)], 1)
-    for a in range(2):
-        second(pf[a], 1 + a, own, True)
-    t.wait_ge(s.aw2, n_w2)
-    for a in range(2):
-        t.wait_ge(s["qh%d" % (3 + a)], 1)
-        second(pf[a], 3 + a, far, False).then_inc(s["p%d" % a], 1)
-    first(5, far, (T.xq, T.xs))
-    t.wait_ge(s.qh5, 1)
-    second(pown, 5, far, False).then_inc(s.pown, 1)
+    rows_read(0, "oo")
+    second(pown, "oo", True)
+    landed("xbs", "xbc")
+    first("ob")
+    rows_read(1, "oo")
+    rows_read(0, "oa")
+    first("pb")
+    rows_read(1, "oa")
+    second(pf[0], "oa", True)
+    landed("w2c", "w2s")
+    second(pf[0], "pa", False).then_inc(s.p0, 1)
+    rows_read(0, "pa")
+    second(pf[1], "ob", True)
+    second(pf[1], "pb", False).then_inc(s.p1, 1)
+    first("po")
+    second(pown, "po", False).then_inc(s.pown, 1)
 
-    sc = g.scalar
+    v, sc = g.vector, g.scalar
     RELU, COPY = ActivationFunctionType.Relu, ActivationFunctionType.Copy
 
-    def tile(k):
-        h = T["h%d" % k]
-        v.wait_ge(s["z0_%d" % k], 1)
+    def rows(k):
+        h = T["h" + k]
+        v.wait_ge(s["z0" + k], 1)
         for b, c in ((0, C), (1, -C)):
-            v.tensor_scalar(h[:, b:512:4], zbank[k][0][:, 0:128], c, 0.0, AluOpType.mult, AluOpType.max).then_inc(s["rv%d" % k], 1)
-        sc.wait_ge(s["z1_%d" % k], 1)
+            v.tensor_scalar(h[:, b:512:4], zbank[k][0][:, 0:128], c, 0.0, AluOpType.mult, AluOpType.max).then_inc(s["r0" + k], 1)
+        sc.wait_ge(s["z1" + k], 1)
         for b, c in ((2, C), (3, -C)):
-            sc.activation(h[:, b:512:4], zbank[k][1][:, 0:128], RELU, scale=c).then_inc(s["rs%d" % k], 1)
-        v.wait_ge(s["rv%d" % k], 2)
-        v.wait_ge(s["rs%d" % k], 2)
-        v.quantize_mx(T["hq%d" % k][:], T["hs%d" % k][:], h[:]).then_inc(s["qh%d" % k], 1)
+            sc.activation(h[:, b:512:4], zbank[k][1][:, 0:128], RELU, scale=c).then_inc(s["r1" + k], 1)
 
-    for k in (0, 1 + early, 1 + late, 3, 4):
-        tile(k)
+    def pack(k):
+        v.wait_ge(s["r0" + k], 2)
+        v.wait_ge(s["r1" + k], 2)
+        v.quantize_mx(T["hq" + k][:], T["hs" + k][:], T["h" + k][:]).then_inc(s["qh" + k], 1)
+
+    v.wait_ge(s.lx, 16)
+    v.quantize_mx(T.xq[:], T.xs[:], T.xb[:]).then_inc(s.qx, 1)
+    v.wait_ge(s.lw1, 16)
+    v.quantize_mx(T.wq[:, 0:256], T.ws[:, 0:256], T.w1b[:]).then_inc(s.qw1, 1)
+    v.wait_ge(s.lw2, 16)
+    v.quantize_mx(T.wq[:, 256:384], T.ws[:, 256:384], T.w2b[:]).then_inc(s.qw2, 1)
+    for k in ("oo", "oa", "pa"):
+        rows(k)
+        pack(k)
+    rows("ob")
+    rows("pb")
+    pack("ob")
+    pack("pb")
     sc.wait_ge(s.p0, 1)
     sc.activation(T.part0[:], pf[0][:, 0:128], COPY).then_inc(s.c0, 1)
     v.wait_ge(s.p1, 1)
     v.tensor_copy(T.part1[:], pf[1][:, 0:128]).then_inc(s.c1, 1)
-    tile(5)
+    rows("po")
+    pack("po")
 
     v.wait_ge(s.pown, 1)
-    v.wait_ge(s["ay%d" % early], n_x)
-    v.tensor_tensor(T.acc[:], pown[:, 0:128], T["land%d" % early][:], AluOpType.add).then_inc(s.added, 1)
+    v.wait_ge(s.ay0, count(topo.mask(next_core, core)))
+    v.tensor_tensor(T.acc[:], pown[:, 0:128], T.land0[:], AluOpType.add).then_inc(s.added, 1)
     v.wait_ge(s.added, 1)
-    v.wait_ge(s["ay%d" % late], n_x)
-    v.tensor_tensor(T.yv[:], T.acc[:], T["land%d" % late][:], AluOpType.add).then_inc(s.yd, 1)
+    v.wait_ge(s.ay1, count(topo.mask(prev_core, core)))
+    v.tensor_tensor(T.yv[:], T.acc[:], T.land1[:], AluOpType.add).then_inc(s.yd, 1)
     g.sync.wait_ge(s.yd, 1)
     g.sync.dma_start(T.y[:], T.yv[:]).then_inc(s.st, 16)
     g.sync.wait_ge(s.st, 16)

from concourse.bass import DstId, RemoteDMATransfer
from concourse.mybir import dt, AluOpType, ActivationFunctionType

F8 = "float8_e4m3fn_x4"
C = 0.023
BLOCKS = ["oo", "oa", "ob", "pa", "pb", "po"]
PIECES = ["xac", "xas", "xbc", "xbs", "w1c0", "w1c1", "w2c", "w1s", "w2s"]

SCRATCH = {
    "xb": ("sbuf", [128, 512], "bfloat16"),
    "w1b": ("sbuf", [128, 1024], "bfloat16"),
    "w2b": ("sbuf", [128, 512], "bfloat16"),
    "xq": ("sbuf", [128, 128], F8), "xs": ("sbuf", [128, 128], "uint8"),
    "fq": ("sbuf", [128, 256], F8), "fs": ("sbuf", [128, 256], "uint8"),
    "wq": ("sbuf", [128, 384], F8), "ws": ("sbuf", [128, 384], "uint8"),
    "mq": ("sbuf", [128, 384], F8), "ms": ("sbuf", [128, 384], "uint8"),
    "part0": ("sbuf", [128, 128], "float32"), "part1": ("sbuf", [128, 128], "float32"),
    "land0": ("sbuf", [128, 128], "float32"), "land1": ("sbuf", [128, 128], "float32"),
    "acc": ("sbuf", [128, 128], "float32"), "yv": ("sbuf", [128, 128], "float32"),
}
SEMAPHORES = ["lx", "lw1", "lw2", "qx", "qw1", "qw2", "ay0", "ay1", "sent", "hop_xbs", "hop_xbc", "p0", "p1",
              "pown", "c0", "c1", "added", "yd", "st"]
SEMAPHORES += ["in_" + _p for _p in PIECES]
for _k in BLOCKS:
    SCRATCH["h" + _k] = ("sbuf", [128, 512], "bfloat16")
    SCRATCH["hq" + _k] = ("sbuf", [128, 128], F8)
    SCRATCH["hs" + _k] = ("sbuf", [128, 128], "uint8")
    SEMAPHORES += [_n + _k for _n in ("z0", "z1", "r0", "r1", "qh")]
for _k in range(8):
    SCRATCH["b%d" % _k] = ("psum", [128, 512], "float32")


def plan(T, topo):
    chips = [topo.chip(c) for c in T.cores]
    n = len(chips)
    group = [[j for j in range(n) if j == i or topo.same_plane(chips[i], chips[j])] for i in range(n)]
    nxt = [group[i][(group[i].index(i) + 1) % len(group[i])] for i in range(n)]
    prv = [group[i][group[i].index(i) - 1] for i in range(n)]
    partner, helper = {}, {}
    for i in range(n):
        for j in range(n):
            if topo.mates(chips[i], chips[j]):
                partner[i] = j
    left = [i for i in range(n) if i not in partner]
    for i in left:
        partner[i] = [j for j in left if j not in group[i]][0]
    for i in range(n):
        c = T.cores[i]
        helper[i] = [k for k in range(128) if topo.chip(k) == chips[i] and topo.die(k) != topo.die(c)
                     and topo.may_write(k, T.cores[prv[i]])][0]
    return nxt, prv, partner, helper


def count(mask):
    return bin(mask).count("1")


def codes(buf, a, b):
    return buf[:, a:b].bitcast(dt.uint8)


def piece(T, p):
    return {"xac": (codes(T.xq, 0, 128), codes(T.fq, 0, 128)), "xas": (T.xs[:], T.fs[:, 0:128]),
            "xbc": (codes(T.xq, 0, 128), codes(T.fq, 128, 256)), "xbs": (T.xs[:], T.fs[:, 128:256]),
            "w1c0": (codes(T.wq, 0, 128), codes(T.mq, 0, 128)), "w1c1": (codes(T.wq, 128, 256), codes(T.mq, 128, 256)),
            "w2c": (codes(T.wq, 256, 384), codes(T.mq, 256, 384)),
            "w1s": (T.ws[:, 0:256], T.ms[:, 0:256]), "w2s": (T.ws[:, 256:384], T.ms[:, 256:384])}[p]


def rank_program(g, core, T, topo):
    rank = T.rank_of(core)
    s = T.sem
    nxt, prv, partner, helper = plan(T, topo)
    sent = []

    def send(*writes):
        transfers = []
        for src, dst, dest, mask, sem in writes:
            a = topo.addr(dest)
            transfers.append(RemoteDMATransfer(srcs=[src], dsts=[dst], dst_ids=[DstId(rid=a[0], pnc=a[1])],
                                               dma_engine_mask=mask, remote_sem=sem, alu_op=0))
            sent.append(count(mask))
        g.remote_dma_fused(transfers, local_sem=s.sent)

    def hop_mask(i):
        free = topo.mask(T.cores[i], helper[i]) & ~topo.mask(T.cores[i], T.cores[partner[i]])
        return sum([1 << e for e in range(free.bit_length()) if free >> e & 1][::2])

    if rank is None:
        for i in helper:
            if helper[i] == core:
                dest = T.cores[prv[i]]
                for p in ("xbs", "xbc"):
                    place = piece(T, p)[1]
                    g.wait_ge(s["hop_" + p], count(hop_mask(i)))
                    send((place, place, dest, topo.mask(core, dest), s["in_" + p]))
                g.wait_ge(s.sent, sum(sent))
        return

    next_core, prev_core, far_core = T.cores[nxt[rank]], T.cores[prv[rank]], T.cores[partner[rank]]

    g.sync.dma_start(T.xb[:], T.x[:]).then_inc(s.lx, 16)
    g.scalar.dma_start(T.w1b[:], T.w1[:]).then_inc(s.lw1, 16)
    g.sync.dma_start(T.w2b[:], T.w2[:]).then_inc(s.lw2, 16)

    def give(p, dest):
        src, dst = piece(T, p)
        return src, dst, dest, topo.mask(core, dest), s["in_" + p]

    def hop(p):
        src, dst = piece(T, p)
        return src, dst, helper[rank], hop_mask(rank), s["hop_" + p]

    g.wait_ge(s.qx, 1)
    send(hop("xbs"))
    send(give("xac", next_core), hop("xbc"))
    send(give("xas", next_core))
    g.wait_ge(s.qw1, 1)
    for p in ("w1c0", "w1s", "w1c1"):
        send(give(p, far_core))
    g.wait_ge(s.qw2, 1)
    for p in ("w2c", "w2s"):
        send(give(p, far_core))
    for a, dest in ((0, prev_core), (1, next_core)):
        g.wait_ge(s["c%d" % a], 1)
        send((T["part%d" % a][:], T["land%d" % a][:], dest, topo.mask(core, dest), s["ay%d" % a]))
    g.wait_ge(s.sent, sum(sent))

    t = g.tensor
    own, far = (T.wq, T.ws), (T.mq, T.ms)
    zbank = {"oo": (T.b0, T.b1), "oa": (T.b2, T.b3), "pa": (T.b4, T.b5), "ob": (T.b6, T.b7), "pb": (T.b1, T.b2),
             "po": (T.b6, T.b7)}
    pown, pf = T.b0, (T.b3, T.b4)

    def landed(*names):
        for p in names:
            sender = {"xa": prev_core, "xb": helper[nxt[rank]]}.get(p[:2], far_core)
            t.wait_ge(s["in_" + p], count(topo.mask(sender, core)))

    def rows_read(i, k):
        t.wait_ge(s["r%d%s" % (i, k)], 2)

    def first(k, tiles=(0, 1)):
        w = own if k[0] == "o" else far
        x = {"o": (T.xq[:], T.xs[:]), "a": (T.fq[:, 0:128], T.fs[:, 0:128]), "b": (T.fq[:, 128:256], T.fs[:, 128:256])}[k[1]]
        for i in tiles:
            t.matmul_mx(zbank[k][i][:, 0:128], w[0][:, 128 * i:128 * i + 128], w[1][:, 128 * i:128 * i + 128],
                        x[0], x[1], True, True).then_inc(s["z%d%s" % (i, k)], 1)

    def second(out, k, start):
        w = own if k[0] == "o" else far
        t.wait_ge(s["qh" + k], 1)
        return t.matmul_mx(out[:, 0:128], w[0][:, 256:384], w[1][:, 256:384], T["hq" + k][:], T["hs" + k][:], start, not start)

    t.wait_ge(s.qx, 1)
    t.wait_ge(s.qw1, 1)
    first("oo")
    landed("xac", "xas")
    first("oa")
    landed("w1c0", "w1s")
    first("pa", (0,))
    landed("w1c1")
    first("pa", (1,))
    t.wait_ge(s.qw2, 1)
    rows_read(0, "oo")
    second(pown, "oo", True)
    landed("xbs", "xbc")
    first("ob")
    rows_read(1, "oo")
    rows_read(0, "oa")
    first("pb")
    rows_read(1, "oa")
    second(pf[0], "oa", True)
    landed("w2c", "w2s")
    second(pf[0], "pa", False).then_inc(s.p0, 1)
    rows_read(0, "pa")
    second(pf[1], "ob", True)
    second(pf[1], "pb", False).then_inc(s.p1, 1)
    first("po")
    second(pown, "po", False).then_inc(s.pown, 1)

    v, sc = g.vector, g.scalar
    RELU, COPY = ActivationFunctionType.Relu, ActivationFunctionType.Copy

    def rows(k):
        h = T["h" + k]
        v.wait_ge(s["z0" + k], 1)
        for b, c in ((0, C), (1, -C)):
            v.tensor_scalar(h[:, b:512:4], zbank[k][0][:, 0:128], c, 0.0, AluOpType.mult, AluOpType.max).then_inc(s["r0" + k], 1)
        sc.wait_ge(s["z1" + k], 1)
        for b, c in ((2, C), (3, -C)):
            sc.activation(h[:, b:512:4], zbank[k][1][:, 0:128], RELU, scale=c).then_inc(s["r1" + k], 1)

    def pack(k):
        v.wait_ge(s["r0" + k], 2)
        v.wait_ge(s["r1" + k], 2)
        v.quantize_mx(T["hq" + k][:], T["hs" + k][:], T["h" + k][:]).then_inc(s["qh" + k], 1)

    v.wait_ge(s.lx, 16)
    v.quantize_mx(T.xq[:], T.xs[:], T.xb[:]).then_inc(s.qx, 1)
    v.wait_ge(s.lw1, 16)
    v.quantize_mx(T.wq[:, 0:256], T.ws[:, 0:256], T.w1b[:]).then_inc(s.qw1, 1)
    v.wait_ge(s.lw2, 16)
    v.quantize_mx(T.wq[:, 256:384], T.ws[:, 256:384], T.w2b[:]).then_inc(s.qw2, 1)
    for k in ("oo", "oa", "pa"):
        rows(k)
        pack(k)
    rows("ob")
    rows("pb")
    pack("ob")
    pack("pb")
    sc.wait_ge(s.p0, 1)
    sc.activation(T.part0[:], pf[0][:, 0:128], COPY).then_inc(s.c0, 1)
    v.wait_ge(s.p1, 1)
    v.tensor_copy(T.part1[:], pf[1][:, 0:128]).then_inc(s.c1, 1)
    rows("po")
    pack("po")

    v.wait_ge(s.pown, 1)
    v.wait_ge(s.ay0, count(topo.mask(next_core, core)))
    v.tensor_tensor(T.acc[:], pown[:, 0:128], T.land0[:], AluOpType.add).then_inc(s.added, 1)
    v.wait_ge(s.added, 1)
    v.wait_ge(s.ay1, count(topo.mask(prev_core, core)))
    v.tensor_tensor(T.yv[:], T.acc[:], T.land1[:], AluOpType.add).then_inc(s.yd, 1)
    g.sync.wait_ge(s.yd, 1)
    g.sync.dma_start(T.y[:], T.yv[:]).then_inc(s.st, 16)
    g.sync.wait_ge(s.st, 16)
